import numpy as np
import ml_dtypes


def mxq(x, axis, fmt="e4m3"):
    dtype, down = {"e4m3": (ml_dtypes.float8_e4m3fn, 7), "e5m2": (ml_dtypes.float8_e5m2, 14)}[fmt]
    v = np.moveaxis(np.asarray(x, np.float32).astype(ml_dtypes.bfloat16).astype(np.float64), axis, -1)
    blocks = v.reshape(v.shape[:-1] + (-1, 32))
    amax = np.abs(blocks).max(-1, keepdims=True)
    byte = np.maximum(np.where(amax > 0, np.frexp(amax)[1] - 1 + 127, 0) - down, 1)
    scale = np.exp2(byte - 127.0)
    codes = (blocks / scale).astype(np.float32).astype(dtype).astype(np.float64)
    return np.moveaxis((codes * scale).reshape(v.shape), -1, axis)


WIDE = False


def mx_kscale(k):
    if not WIDE:
        return np.ones(k)
    levels = np.array([10, -10, 5, -5, 0])
    if k % 512:
        return np.exp2(np.random.permutation(np.resize(levels, k // 32))).repeat(32)
    a = np.empty((k // 512, 16))
    for p in range(k // 512):
        a[p, :8] = np.random.permutation(np.resize(levels, 8))
        for g in range(8):
            far = levels[np.abs(levels - a[p, g]) >= 10]
            a[p, g + 8] = far[np.random.randint(len(far))]
    return np.exp2(a.ravel()).repeat(32)


def f64(x):
    return np.asarray(x).astype(np.float64)


def striped(idx):
    return np.tile(idx.reshape(-1, 16).T, (8, 1)).astype(np.uint16)


def unstriped(offs):
    return offs[:16].T.reshape(-1).astype(np.int64)


def relu(v):
    return np.maximum(v, 0.0)


K, T, E, C, N = 1536, 512, 8, 128, 128


def by_expert(wq, xq):
    return np.concatenate([wq[e].T @ xq[:, e * C:(e + 1) * C] for e in range(E)], axis=1)


def setup_inputs():
    n = np.random.standard_normal
    s = mx_kscale(K)[:, None]
    first = np.random.permutation(np.repeat(np.arange(E), T // E))
    second = (first + 1 + np.random.permutation(np.repeat(np.arange(E - 1), -(-T // (E - 1)))[:T])) % E
    while np.bincount(second, minlength=E).max() != T // E:
        load = np.bincount(second, minlength=E); hi, lo = int(load.argmax()), int(load.argmin())
        t = np.flatnonzero((second == hi) & (first != lo))[0]; second[t] = lo
    slot_token = np.empty(E * C, np.int64); pos = np.empty((2, T), np.int64); fill = np.zeros(E, np.int64)
    place = np.stack([np.random.permutation(C) for _ in range(E)])
    for r, deal in enumerate((first, second)):
        for t in np.random.permutation(T):
            e = deal[t]; j = e * C + place[e, fill[e]]; fill[e] += 1; slot_token[j] = t; pos[r, t] = j
    g = np.random.uniform(0.2, 0.8, T)
    return {
        "xT": (n((K, T)) * s).astype(np.float32),
        "w": (n((E, K, N)) / np.sqrt(K) / s[None]).astype(np.float32),
        "b": (0.3 * n((N, E))).astype(np.float32),
        "gate": np.stack([np.tile(g, (N, 1)), np.tile(1.0 - g, (N, 1))]).astype(np.float32),
        "offs": striped(slot_token),
        "pos1": striped(pos[0]),
        "pos2": striped(pos[1]),
    }


def reference(xT, w, b, gate, offs, pos1, pos2):
    idx = unstriped(offs)
    xq = mxq(f64(xT)[:, idx], 0, "e4m3")
    y = by_expert(mxq(f64(w), 1, "e4m3"), xq)
    y = relu(y + np.repeat(f64(b), C, axis=1))
    return f64(gate[0]) * y[:, unstriped(pos1)] + f64(gate[1]) * y[:, unstriped(pos2)]

@@ -1,0 +1,139 @@
+from contextlib import ExitStack
+
+import concourse.mybir as mybir
+
+K, T, E, C, N = 1536, 512, 8, 128, 128
+P = 128
+PACK = 4
+PASS = P * PACK
+A = K // PASS
+SLOTS = E * C
+W_PAD = 1408
+
+FLOPS = 2 * K * N * SLOTS
+
+F32 = mybir.dt.float32
+BF16 = mybir.dt.bfloat16
+I32 = mybir.dt.int32
+U32 = mybir.dt.uint32
+U16 = mybir.dt.uint16
+U8 = mybir.dt.uint8
+FP8X4 = mybir.dt.float8_e4m3fn_x4
+RELU = mybir.ActivationFunctionType.Relu
+ADD = mybir.AluOpType.add
+MULT = mybir.AluOpType.mult
+
+W_CHUNKS = [4] * 5 + [2, 1, 1]
+W_ENGINE = "SSSSSVVV"
+REUSED = 3
+X_CUT = (256, 192, 192)
+
+
+def tile_routed_moe_kernel(tc, xT, w, b, gate, offs, pos1, pos2, out):
+    nc = tc.nc
+    with ExitStack() as ctx:
+        keep = ctx.enter_context(tc.tile_pool(name="keep", bufs=1))
+        psum = ctx.enter_context(tc.psum_pool(name="psum", bufs=1))
+
+        offs_t = keep.tile([P, SLOTS // 16], U16, name="offs_t")
+        pos1_t = keep.tile([P, T // 16], U16, name="pos1_t")
+        pos2_t = keep.tile([P, T // 16], U16, name="pos2_t")
+        bias = keep.tile([P, E], F32, name="bias")
+        gates = keep.tile([P, 2, T], F32, name="gates")
+
+        x_view = xT.rearrange("(a p t) n -> a p t n", p=P, t=PACK)
+        w_view = w.flatten_outer_dims().rearrange("(u p t) n -> p u (t n)", p=P, t=PACK)
+
+        x_raw = {}
+        for a in range(A):
+            cuts = [0, X_CUT[0], T] if a == 0 else [0, T]
+            for lo, hi in zip(cuts[:-1], cuts[1:]):
+                raw = keep.tile([P, PACK, hi - lo], F32, name=f"x_raw_{a}_{lo}")
+                nc.sync.dma_start(out=raw[:], in_=x_view[a][:, :, lo:hi])
+                x_raw[a, lo] = raw
+            if a == 0:
+                nc.sync.dma_start(offs_t[:], offs)
+        nc.sync.dma_start(out=bias[:], in_=b)
+        w_raw = []
+        first = 0
+        for i, units in enumerate(W_CHUNKS):
+            raw = keep.tile([P, units, PACK * N], F32, name=f"w_raw_{i}", tag="reused" if i == REUSED else f"w_raw_{i}")
+            nc.sync.dma_start(out=raw[:], in_=w_view[:, first : first + units, :])
+            w_raw.append(raw)
+            first += units
+            if i == 2:
+                nc.sync.dma_start(pos1_t[:], pos1)
+                nc.sync.dma_start(pos2_t[:], pos2)
+        nc.sync.dma_start(out=gates[:], in_=gate.rearrange("r n t -> n r t"))
+
+        x_scales = keep.tile([P, W_PAD], U8, name="x_scales", align_bytes=64)
+        nc.gpsimd.memset(x_scales[:], 0)
+        x_words = []
+        for a in range(A):
+            words = keep.tile([P, W_PAD], U32, name=f"x_words_{a}", align_bytes=64)
+            nc.vector.memset(words[:, T:W_PAD].bitcast(I32), 0)
+            x_words.append(words)
+
+        slot_words = keep.tile([P, A, SLOTS], U32, name="slot_words", align_bytes=64)
+        slot_scales = keep.tile([P, SLOTS], U8, name="slot_scales", align_bytes=64)
+        for a in range(A):
+            grouped = keep.tile([P, T, PACK], BF16, name=f"x_grouped_{a}", align_bytes=64)
+            for lo, hi, copy in ((0, X_CUT[a], nc.vector.tensor_copy), (X_CUT[a], T, nc.scalar.copy)):
+                src = x_raw[a, lo][:] if a == 0 else x_raw[a, 0][:, :, lo:hi]
+                copy(out=grouped[:, lo:hi, :], in_=src.rearrange("p t n -> p n t"))
+            cuts = [0, X_CUT[0], T] if a == 0 else [0, T]
+            for lo, hi in zip(cuts[:-1], cuts[1:]):
+                nc.vector.quantize_mx(
+                    out=x_words[a][:, lo:hi].bitcast(FP8X4),
+                    scales=x_scales[4 * a : P, lo:hi],
+                    in_=grouped[:, lo:hi, :].rearrange("p n t -> p (n t)"),
+                )
+            nc.vector.tensor_copy(slot_words[:, a, :], x_words[a][:].indirect(offs_t[:]))
+        nc.vector.tensor_copy(slot_scales[:], x_scales[:].indirect(offs_t[:]))
+
+        w_words, w_scales = [], []
+        done = 0
+        acc = None
+        sums = []
+        for i, units in enumerate(W_CHUNKS):
+            grouped = keep.tile([P, units, N, PACK], BF16, name=f"w_grouped_{i}", align_bytes=64)
+            copy = nc.vector.tensor_copy if W_ENGINE[i] == "V" else nc.scalar.copy
+            copy(out=grouped[:], in_=w_raw[i][:].rearrange("p u (t n) -> p u n t", t=PACK))
+            words = keep.tile([P, units * N], U32, name=f"w_words_{i}", align_bytes=64)
+            scales = keep.tile([P, units * N], U8, name=f"w_scales_{i}", align_bytes=64)
+            nc.vector.quantize_mx(
+                out=words[:].bitcast(FP8X4), scales=scales[:], in_=grouped[:].rearrange("p u n t -> p (u n t)")
+            )
+            for j in range(units):
+                e, a = divmod(done, A)
+                if a == 0:
+                    acc = psum.tile([N, C], F32, name=f"acc_{e}")
+                cols = slice(j * N, (j + 1) * N)
+                sl = slice(e * C, (e + 1) * C)
+                nc.tensor.matmul_mx(
+                    out=acc[:],
+                    lhsT=words[:, cols].bitcast(FP8X4),
+                    lhsT_scale=scales[:, cols],
+                    rhs=slot_words[:, a, sl].bitcast(FP8X4),
+                    rhs_scale=slot_scales[4 * a : P, sl],
+                    start=(a == 0),
+                    stop=(a == A - 1),
+                )
+                if a == A - 1:
+                    sums.append(acc)
+                done += 1
+        slots = keep.tile([P, SLOTS], F32, name="slots", tag="reused")
+        for e in range(E):
+            nc.scalar.activation(slots[:, e * C : (e + 1) * C], sums[e][:], RELU, bias=bias[:, e : e + 1])
+
+        H = T // 2
+        for h in range(2):
+            t0 = slice(h * H, (h + 1) * H)
+            o = slice(h * H // 16, (h + 1) * H // 16)
+            y1 = keep.tile([P, H], F32, name=f"y1_{h}")
+            y2 = keep.tile([P, H], F32, name=f"y2_{h}")
+            y = keep.tile([P, H], F32, name=f"y_{h}")
+            nc.vector.tensor_tensor(y1[:], slots[:].indirect(pos1_t[:, o]), gates[:, 0, t0], MULT)
+            nc.vector.tensor_tensor(y2[:], slots[:].indirect(pos2_t[:, o]), gates[:, 1, t0], MULT)
+            nc.vector.tensor_tensor(y[:], y1[:], y2[:], ADD)
+            nc.sync.dma_start(out=out[:, t0], in_=y[:])

@@ -80,7 +80,10 @@ def tile_routed_moe_kernel(tc, xT, w, b, gate, offs, pos1, pos2, out):
             grouped = keep.tile([P, T, PACK], BF16, name=f"x_grouped_{a}", align_bytes=64)
             for lo, hi, copy in ((0, X_CUT[a], nc.vector.tensor_copy), (X_CUT[a], T, nc.scalar.copy)):
                 src = x_raw[a, lo][:] if a == 0 else x_raw[a, 0][:, :, lo:hi]
-                copy(out=grouped[:, lo:hi, :], in_=src.rearrange("p t n -> p n t"))
+                copy(
+                    out=grouped[:, lo:hi, :].rearrange("p (c i) t -> p c t i", i=4),
+                    in_=src.rearrange("p t (c i) -> p c t i", i=4),
+                )
             cuts = [0, X_CUT[0], T] if a == 0 else [0, T]
             for lo, hi in zip(cuts[:-1], cuts[1:]):
                 nc.vector.quantize_mx(
@@ -98,7 +101,10 @@ def tile_routed_moe_kernel(tc, xT, w, b, gate, offs, pos1, pos2, out):
         for i, units in enumerate(W_CHUNKS):
             grouped = keep.tile([P, units, N, PACK], BF16, name=f"w_grouped_{i}", align_bytes=64)
             copy = nc.vector.tensor_copy if W_ENGINE[i] == "V" else nc.scalar.copy
-            copy(out=grouped[:], in_=w_raw[i][:].rearrange("p u (t n) -> p u n t", t=PACK))
+            copy(
+                out=grouped[:].rearrange("p u (c i) t -> p u c t i", i=4),
+                in_=w_raw[i][:].rearrange("p u (t c i) -> p u c t i", t=PACK, i=4),
+            )
             words = keep.tile([P, units * N], U32, name=f"w_words_{i}", align_bytes=64)
             scales = keep.tile([P, units * N], U8, name=f"w_scales_{i}", align_bytes=64)
             nc.vector.quantize_mx(

@@ -24,13 +24,21 @@ ADD = mybir.AluOpType.add
 MULT = mybir.AluOpType.mult
 
 W_CHUNKS = [4] * 5 + [2, 1, 1]
-W_ENGINE = "SSSSSVVV"
-REUSED = 3
-X_CUT = (256, 192, 192)
+S3G = (("S", 0, 3), ("G", 3, 4))
+W_SPLIT = [(("S", 0, 4),), S3G, S3G, S3G, (("S", 0, 3), ("V", 3, 4)), (("V", 0, 2),), (("V", 0, 1),), (("V", 0, 1),)]
+REUSED = 4
+OUT_CUTS = ((0, 320), (320, 512))
+X_CHUNKS = (((0, 256), (256, 384), (384, 512)), ((0, 512),), ((0, 512),))
+X_SPLIT = (
+    (("V", 0, 256), ("V", 256, 384), ("V", 384, 512)),
+    (("S", 0, 384), ("V", 384, 512)),
+    (("S", 0, 512),),
+)
 
 
 def tile_routed_moe_kernel(tc, xT, w, b, gate, offs, pos1, pos2, out):
     nc = tc.nc
+    engine_copy = {"V": nc.vector.tensor_copy, "S": nc.scalar.copy, "G": nc.gpsimd.tensor_copy}
     with ExitStack() as ctx:
         keep = ctx.enter_context(tc.tile_pool(name="keep", bufs=1))
         psum = ctx.enter_context(tc.psum_pool(name="psum", bufs=1))
@@ -46,8 +54,7 @@ def tile_routed_moe_kernel(tc, xT, w, b, gate, offs, pos1, pos2, out):
 
         x_raw = {}
         for a in range(A):
-            cuts = [0, X_CUT[0], T] if a == 0 else [0, T]
-            for lo, hi in zip(cuts[:-1], cuts[1:]):
+            for lo, hi in X_CHUNKS[a]:
                 raw = keep.tile([P, PACK, hi - lo], F32, name=f"x_raw_{a}_{lo}")
                 nc.sync.dma_start(out=raw[:], in_=x_view[a][:, :, lo:hi])
                 x_raw[a, lo] = raw
@@ -78,14 +85,13 @@ def tile_routed_moe_kernel(tc, xT, w, b, gate, offs, pos1, pos2, out):
         slot_scales = keep.tile([P, SLOTS], U8, name="slot_scales", align_bytes=64)
         for a in range(A):
             grouped = keep.tile([P, T, PACK], BF16, name=f"x_grouped_{a}", align_bytes=64)
-            for lo, hi, copy in ((0, X_CUT[a], nc.vector.tensor_copy), (X_CUT[a], T, nc.scalar.copy)):
+            for copy, lo, hi in X_SPLIT[a]:
                 src = x_raw[a, lo][:] if a == 0 else x_raw[a, 0][:, :, lo:hi]
-                copy(
+                engine_copy[copy](
                     out=grouped[:, lo:hi, :].rearrange("p (c i) t -> p c t i", i=4),
                     in_=src.rearrange("p t (c i) -> p c t i", i=4),
                 )
-            cuts = [0, X_CUT[0], T] if a == 0 else [0, T]
-            for lo, hi in zip(cuts[:-1], cuts[1:]):
+            for lo, hi in X_CHUNKS[a]:
                 nc.vector.quantize_mx(
                     out=x_words[a][:, lo:hi].bitcast(FP8X4),
                     scales=x_scales[4 * a : P, lo:hi],
@@ -100,11 +106,11 @@ def tile_routed_moe_kernel(tc, xT, w, b, gate, offs, pos1, pos2, out):
         sums = []
         for i, units in enumerate(W_CHUNKS):
             grouped = keep.tile([P, units, N, PACK], BF16, name=f"w_grouped_{i}", align_bytes=64)
-            copy = nc.vector.tensor_copy if W_ENGINE[i] == "V" else nc.scalar.copy
-            copy(
-                out=grouped[:].rearrange("p u (c i) t -> p u c t i", i=4),
-                in_=w_raw[i][:].rearrange("p u (t c i) -> p u c t i", t=PACK, i=4),
-            )
+            for copy, u0, u1 in W_SPLIT[i]:
+                engine_copy[copy](
+                    out=grouped[:, u0:u1].rearrange("p u (c i) t -> p u c t i", i=4),
+                    in_=w_raw[i][:, u0:u1].rearrange("p u (t c i) -> p u c t i", t=PACK, i=4),
+                )
             words = keep.tile([P, units * N], U32, name=f"w_words_{i}", align_bytes=64)
             scales = keep.tile([P, units * N], U8, name=f"w_scales_{i}", align_bytes=64)
             nc.vector.quantize_mx(
@@ -132,14 +138,14 @@ def tile_routed_moe_kernel(tc, xT, w, b, gate, offs, pos1, pos2, out):
         for e in range(E):
             nc.scalar.activation(slots[:, e * C : (e + 1) * C], sums[e][:], RELU, bias=bias[:, e : e + 1])
 
-        H = T // 2
-        for h in range(2):
-            t0 = slice(h * H, (h + 1) * H)
-            o = slice(h * H // 16, (h + 1) * H // 16)
-            y1 = keep.tile([P, H], F32, name=f"y1_{h}")
-            y2 = keep.tile([P, H], F32, name=f"y2_{h}")
-            y = keep.tile([P, H], F32, name=f"y_{h}")
-            nc.vector.tensor_tensor(y1[:], slots[:].indirect(pos1_t[:, o]), gates[:, 0, t0], MULT)
-            nc.vector.tensor_tensor(y2[:], slots[:].indirect(pos2_t[:, o]), gates[:, 1, t0], MULT)
-            nc.vector.tensor_tensor(y[:], y1[:], y2[:], ADD)
-            nc.sync.dma_start(out=out[:, t0], in_=y[:])
+        y1 = keep.tile([P, T], F32, name="y1")
+        nc.vector.tensor_tensor(y1[:], slots[:].indirect(pos1_t[:]), gates[:, 0, :], MULT)
+        y2s = []
+        for t0, t1 in OUT_CUTS:
+            y2 = keep.tile([P, t1 - t0], F32, name=f"y2_{t0}")
+            nc.vector.tensor_tensor(y2[:], slots[:].indirect(pos2_t[:, t0 // 16 : t1 // 16]), gates[:, 1, t0:t1], MULT)
+            y2s.append(y2)
+        for (t0, t1), y2 in zip(OUT_CUTS, y2s):
+            y = keep.tile([P, t1 - t0], F32, name=f"y_{t0}")
+            nc.vector.tensor_tensor(y[:], y1[:, t0:t1], y2[:], ADD)
+            nc.sync.dma_start(out=out[:, t0:t1], in_=y[:])

@@ -24,13 +24,14 @@ ADD = mybir.AluOpType.add
 MULT = mybir.AluOpType.mult
 
 W_CHUNKS = [4] * 5 + [2, 1, 1]
-S3G = (("S", 0, 3), ("G", 3, 4))
-W_SPLIT = [(("S", 0, 4),), S3G, S3G, S3G, (("S", 0, 3), ("V", 3, 4)), (("V", 0, 2),), (("V", 0, 1),), (("V", 0, 1),)]
+S4 = (("S", 0, 4),)
+S3V = (("S", 0, 3), ("V", 3, 4))
+W_SPLIT = [S4, S4, S4, S3V, S4, (("V", 0, 2),), (("V", 0, 1),), (("V", 0, 1),)]
 REUSED = 4
 OUT_CUTS = ((0, 320), (320, 512))
-X_CHUNKS = (((0, 256), (256, 384), (384, 512)), ((0, 512),), ((0, 512),))
+X_CHUNKS = (((0, 512),), ((0, 512),), ((0, 512),))
 X_SPLIT = (
-    (("V", 0, 256), ("V", 256, 384), ("V", 384, 512)),
+    (("V", 0, 320), ("S", 320, 512)),
     (("S", 0, 384), ("V", 384, 512)),
     (("S", 0, 512),),
 )
@@ -86,7 +87,7 @@ def tile_routed_moe_kernel(tc, xT, w, b, gate, offs, pos1, pos2, out):
         for a in range(A):
             grouped = keep.tile([P, T, PACK], BF16, name=f"x_grouped_{a}", align_bytes=64)
             for copy, lo, hi in X_SPLIT[a]:
-                src = x_raw[a, lo][:] if a == 0 else x_raw[a, 0][:, :, lo:hi]
+                src = x_raw[a, 0][:, :, lo:hi]
                 engine_copy[copy](
                     out=grouped[:, lo:hi, :].rearrange("p (c i) t -> p c t i", i=4),
                     in_=src.rearrange("p t (c i) -> p c t i", i=4),

@@ -5,10 +5,8 @@ import concourse.mybir as mybir
 K, T, E, C, N = 1536, 512, 8, 128, 128
 P = 128
 PACK = 4
-PASS = P * PACK
-A = K // PASS
+A = K // (P * PACK)
 SLOTS = E * C
-W_PAD = 1408
 
 FLOPS = 2 * K * N * SLOTS
 
@@ -21,132 +19,144 @@ U8 = mybir.dt.uint8
 FP8X4 = mybir.dt.float8_e4m3fn_x4
 RELU = mybir.ActivationFunctionType.Relu
 ADD = mybir.AluOpType.add
+MAX = mybir.AluOpType.max
 MULT = mybir.AluOpType.mult
 
-W_CHUNKS = [4] * 5 + [2, 1, 1]
-S4 = (("S", 0, 4),)
-S3V = (("S", 0, 3), ("V", 3, 4))
-W_SPLIT = [S4, S4, S4, S3V, S4, (("V", 0, 2),), (("V", 0, 1),), (("V", 0, 1),)]
-REUSED = 4
-OUT_CUTS = ((0, 320), (320, 512))
-X_CHUNKS = (((0, 512),), ((0, 512),), ((0, 512),))
-X_SPLIT = (
-    (("V", 0, 320), ("S", 320, 512)),
-    (("S", 0, 384), ("V", 384, 512)),
-    (("S", 0, 512),),
+WINDOW = 1408
+
+SCALE_ROW = 4
+
+X_SHARES = (
+    (("vector", 0, 320), ("scalar", 320, 512)),
+    (("scalar", 0, 384), ("vector", 384, 512)),
+    (("scalar", 0, 512),),
 )
+
+W_GROUPS = ((4, 0), (4, 0), (4, 0), (3, 1), (2, 0), (0, 2), (0, 2), (0, 1), (0, 1))
+
+REUSED_GROUP = 4
+
+POS_AFTER_GROUP = 2
+
+OUT_CUTS = ((0, 320), (320, 512))
 
 
 def tile_routed_moe_kernel(tc, xT, w, b, gate, offs, pos1, pos2, out):
     nc = tc.nc
-    engine_copy = {"V": nc.vector.tensor_copy, "S": nc.scalar.copy, "G": nc.gpsimd.tensor_copy}
+    engine_copy = {"vector": nc.vector.tensor_copy, "scalar": nc.scalar.copy}
+
     with ExitStack() as ctx:
         keep = ctx.enter_context(tc.tile_pool(name="keep", bufs=1))
         psum = ctx.enter_context(tc.psum_pool(name="psum", bufs=1))
 
-        offs_t = keep.tile([P, SLOTS // 16], U16, name="offs_t")
-        pos1_t = keep.tile([P, T // 16], U16, name="pos1_t")
-        pos2_t = keep.tile([P, T // 16], U16, name="pos2_t")
+        offs_tile = keep.tile([P, SLOTS // 16], U16, name="offs_tile")
+        pos1_tile = keep.tile([P, T // 16], U16, name="pos1_tile")
+        pos2_tile = keep.tile([P, T // 16], U16, name="pos2_tile")
         bias = keep.tile([P, E], F32, name="bias")
         gates = keep.tile([P, 2, T], F32, name="gates")
 
-        x_view = xT.rearrange("(a p t) n -> a p t n", p=P, t=PACK)
-        w_view = w.flatten_outer_dims().rearrange("(u p t) n -> p u (t n)", p=P, t=PACK)
-
-        x_raw = {}
+        x_rows = xT.rearrange("(a p t) n -> a p t n", p=P, t=PACK)
+        x_raw = []
         for a in range(A):
-            for lo, hi in X_CHUNKS[a]:
-                raw = keep.tile([P, PACK, hi - lo], F32, name=f"x_raw_{a}_{lo}")
-                nc.sync.dma_start(out=raw[:], in_=x_view[a][:, :, lo:hi])
-                x_raw[a, lo] = raw
+            raw = keep.tile([P, PACK, T], F32, name=f"x_raw_{a}")
+            nc.sync.dma_start(out=raw[:], in_=x_rows[a])
+            x_raw.append(raw)
             if a == 0:
-                nc.sync.dma_start(offs_t[:], offs)
+                nc.sync.dma_start(offs_tile[:], offs)
         nc.sync.dma_start(out=bias[:], in_=b)
+        w_rows = w.flatten_outer_dims().rearrange("(u p t) n -> p u (t n)", p=P, t=PACK)
         w_raw = []
         first = 0
-        for i, units in enumerate(W_CHUNKS):
-            raw = keep.tile([P, units, PACK * N], F32, name=f"w_raw_{i}", tag="reused" if i == REUSED else f"w_raw_{i}")
-            nc.sync.dma_start(out=raw[:], in_=w_view[:, first : first + units, :])
+        for i, shares in enumerate(W_GROUPS):
+            blocks = sum(shares)
+            tag = "reused" if i == REUSED_GROUP else f"w_raw_{i}"
+            raw = keep.tile([P, blocks, PACK * N], F32, name=f"w_raw_{i}", tag=tag)
+            nc.sync.dma_start(out=raw[:], in_=w_rows[:, first : first + blocks, :])
             w_raw.append(raw)
-            first += units
-            if i == 2:
-                nc.sync.dma_start(pos1_t[:], pos1)
-                nc.sync.dma_start(pos2_t[:], pos2)
+            first += blocks
+            if i == POS_AFTER_GROUP:
+                nc.sync.dma_start(pos1_tile[:], pos1)
+                nc.sync.dma_start(pos2_tile[:], pos2)
         nc.sync.dma_start(out=gates[:], in_=gate.rearrange("r n t -> n r t"))
 
-        x_scales = keep.tile([P, W_PAD], U8, name="x_scales", align_bytes=64)
+        x_scales = keep.tile([P, WINDOW], U8, name="x_scales", align_bytes=64)
         nc.gpsimd.memset(x_scales[:], 0)
         x_words = []
         for a in range(A):
-            words = keep.tile([P, W_PAD], U32, name=f"x_words_{a}", align_bytes=64)
-            nc.vector.memset(words[:, T:W_PAD].bitcast(I32), 0)
+            words = keep.tile([P, WINDOW], U32, name=f"x_words_{a}", align_bytes=64)
+            nc.vector.memset(words[:, T:WINDOW].bitcast(I32), 0)
             x_words.append(words)
 
         slot_words = keep.tile([P, A, SLOTS], U32, name="slot_words", align_bytes=64)
         slot_scales = keep.tile([P, SLOTS], U8, name="slot_scales", align_bytes=64)
         for a in range(A):
             grouped = keep.tile([P, T, PACK], BF16, name=f"x_grouped_{a}", align_bytes=64)
-            for copy, lo, hi in X_SPLIT[a]:
-                src = x_raw[a, 0][:, :, lo:hi]
-                engine_copy[copy](
+            for engine, lo, hi in X_SHARES[a]:
+                engine_copy[engine](
                     out=grouped[:, lo:hi, :].rearrange("p (c i) t -> p c t i", i=4),
-                    in_=src.rearrange("p t (c i) -> p c t i", i=4),
+                    in_=x_raw[a][:, :, lo:hi].rearrange("p t (c i) -> p c t i", i=4),
                 )
-            for lo, hi in X_CHUNKS[a]:
-                nc.vector.quantize_mx(
-                    out=x_words[a][:, lo:hi].bitcast(FP8X4),
-                    scales=x_scales[4 * a : P, lo:hi],
-                    in_=grouped[:, lo:hi, :].rearrange("p n t -> p (n t)"),
-                )
-            nc.vector.tensor_copy(slot_words[:, a, :], x_words[a][:].indirect(offs_t[:]))
-        nc.vector.tensor_copy(slot_scales[:], x_scales[:].indirect(offs_t[:]))
-
-        w_words, w_scales = [], []
-        done = 0
-        acc = None
-        sums = []
-        for i, units in enumerate(W_CHUNKS):
-            grouped = keep.tile([P, units, N, PACK], BF16, name=f"w_grouped_{i}", align_bytes=64)
-            for copy, u0, u1 in W_SPLIT[i]:
-                engine_copy[copy](
-                    out=grouped[:, u0:u1].rearrange("p u (c i) t -> p u c t i", i=4),
-                    in_=w_raw[i][:, u0:u1].rearrange("p u (t c i) -> p u c t i", t=PACK, i=4),
-                )
-            words = keep.tile([P, units * N], U32, name=f"w_words_{i}", align_bytes=64)
-            scales = keep.tile([P, units * N], U8, name=f"w_scales_{i}", align_bytes=64)
             nc.vector.quantize_mx(
-                out=words[:].bitcast(FP8X4), scales=scales[:], in_=grouped[:].rearrange("p u n t -> p (u n t)")
+                out=x_words[a][:, 0:T].bitcast(FP8X4),
+                scales=x_scales[SCALE_ROW * a : P, 0:T],
+                in_=grouped[:].rearrange("p n t -> p (n t)"),
             )
-            for j in range(units):
-                e, a = divmod(done, A)
+            nc.vector.tensor_copy(slot_words[:, a, :], x_words[a][:].indirect(offs_tile[:]))
+        nc.vector.tensor_copy(slot_scales[:], x_scales[:].indirect(offs_tile[:]))
+
+        sums = []
+        block = 0
+        for i, (scalar_blocks, vector_blocks) in enumerate(W_GROUPS):
+            blocks = scalar_blocks + vector_blocks
+            grouped = keep.tile([P, blocks, N, PACK], BF16, name=f"w_grouped_{i}", align_bytes=64)
+            for engine, lo, hi in (("scalar", 0, scalar_blocks), ("vector", scalar_blocks, blocks)):
+                if lo < hi:
+                    engine_copy[engine](
+                        out=grouped[:, lo:hi].rearrange("p u (c i) t -> p u c t i", i=4),
+                        in_=w_raw[i][:, lo:hi].rearrange("p u (t c i) -> p u c t i", t=PACK, i=4),
+                    )
+            w_words = keep.tile([P, blocks * N], U32, name=f"w_words_{i}", align_bytes=64)
+            w_scales = keep.tile([P, blocks * N], U8, name=f"w_scales_{i}", align_bytes=64)
+            nc.vector.quantize_mx(
+                out=w_words[:].bitcast(FP8X4),
+                scales=w_scales[:],
+                in_=grouped[:].rearrange("p u n t -> p (u n t)"),
+            )
+            for j in range(blocks):
+                e, a = divmod(block, A)
                 if a == 0:
-                    acc = psum.tile([N, C], F32, name=f"acc_{e}")
-                cols = slice(j * N, (j + 1) * N)
-                sl = slice(e * C, (e + 1) * C)
+                    sums.append(psum.tile([N, C], F32, name=f"sums_{e}"))
+                features = slice(j * N, (j + 1) * N)
+                places = slice(e * C, (e + 1) * C)
                 nc.tensor.matmul_mx(
-                    out=acc[:],
-                    lhsT=words[:, cols].bitcast(FP8X4),
-                    lhsT_scale=scales[:, cols],
-                    rhs=slot_words[:, a, sl].bitcast(FP8X4),
-                    rhs_scale=slot_scales[4 * a : P, sl],
+                    out=sums[e][:],
+                    lhsT=w_words[:, features].bitcast(FP8X4),
+                    lhsT_scale=w_scales[:, features],
+                    rhs=slot_words[:, a, places].bitcast(FP8X4),
+                    rhs_scale=slot_scales[SCALE_ROW * a : P, places],
                     start=(a == 0),
                     stop=(a == A - 1),
                 )
-                if a == A - 1:
-                    sums.append(acc)
-                done += 1
-        slots = keep.tile([P, SLOTS], F32, name="slots", tag="reused")
+                block += 1
+
+        results = keep.tile([P, SLOTS], F32, name="results", tag="reused")
         for e in range(E):
-            nc.scalar.activation(slots[:, e * C : (e + 1) * C], sums[e][:], RELU, bias=bias[:, e : e + 1])
+            places = slice(e * C, (e + 1) * C)
+            if e < E - 1:
+                nc.scalar.activation(results[:, places], sums[e][:], RELU, bias=bias[:, e : e + 1])
+            else:
+                nc.vector.tensor_scalar(results[:, places], sums[e][:], bias[:, e : e + 1], 0.0, ADD, MAX)
 
         y1 = keep.tile([P, T], F32, name="y1")
-        nc.vector.tensor_tensor(y1[:], slots[:].indirect(pos1_t[:]), gates[:, 0, :], MULT)
-        y2s = []
-        for t0, t1 in OUT_CUTS:
-            y2 = keep.tile([P, t1 - t0], F32, name=f"y2_{t0}")
-            nc.vector.tensor_tensor(y2[:], slots[:].indirect(pos2_t[:, t0 // 16 : t1 // 16]), gates[:, 1, t0:t1], MULT)
-            y2s.append(y2)
-        for (t0, t1), y2 in zip(OUT_CUTS, y2s):
-            y = keep.tile([P, t1 - t0], F32, name=f"y_{t0}")
-            nc.vector.tensor_tensor(y[:], y1[:, t0:t1], y2[:], ADD)
-            nc.sync.dma_start(out=out[:, t0:t1], in_=y[:])
+        nc.vector.tensor_tensor(y1[:], results[:].indirect(pos1_tile[:]), gates[:, 0, :], MULT)
+        y2 = []
+        for lo, hi in OUT_CUTS:
+            part = keep.tile([P, hi - lo], F32, name=f"y2_{lo}")
+            nc.vector.tensor_tensor(
+                part[:], results[:].indirect(pos2_tile[:, lo // 16 : hi // 16]), gates[:, 1, lo:hi], MULT
+            )
+            y2.append(part)
+        for (lo, hi), part in zip(OUT_CUTS, y2):
+            y = keep.tile([P, hi - lo], F32, name=f"y_{lo}")
+            nc.vector.tensor_tensor(y[:], y1[:, lo:hi], part[:], ADD)
+            nc.sync.dma_start(out=out[:, lo:hi], in_=y[:])

from contextlib import ExitStack

import concourse.mybir as mybir

K, T, E, C, N = 1536, 512, 8, 128, 128
P = 128
PACK = 4
A = K // (P * PACK)
SLOTS = E * C

FLOPS = 2 * K * N * SLOTS

F32 = mybir.dt.float32
BF16 = mybir.dt.bfloat16
I32 = mybir.dt.int32
U32 = mybir.dt.uint32
U16 = mybir.dt.uint16
U8 = mybir.dt.uint8
FP8X4 = mybir.dt.float8_e4m3fn_x4
RELU = mybir.ActivationFunctionType.Relu
ADD = mybir.AluOpType.add
MAX = mybir.AluOpType.max
MULT = mybir.AluOpType.mult

WINDOW = 1408

SCALE_ROW = 4

X_SHARES = (
    (("vector", 0, 320), ("scalar", 320, 512)),
    (("scalar", 0, 384), ("vector", 384, 512)),
    (("scalar", 0, 512),),
)

W_GROUPS = ((4, 0), (4, 0), (4, 0), (3, 1), (2, 0), (0, 2), (0, 2), (0, 1), (0, 1))

REUSED_GROUP = 4

POS_AFTER_GROUP = 2

OUT_CUTS = ((0, 320), (320, 512))


def tile_routed_moe_kernel(tc, xT, w, b, gate, offs, pos1, pos2, out):
    nc = tc.nc
    engine_copy = {"vector": nc.vector.tensor_copy, "scalar": nc.scalar.copy}

    with ExitStack() as ctx:
        keep = ctx.enter_context(tc.tile_pool(name="keep", bufs=1))
        psum = ctx.enter_context(tc.psum_pool(name="psum", bufs=1))

        offs_tile = keep.tile([P, SLOTS // 16], U16, name="offs_tile")
        pos1_tile = keep.tile([P, T // 16], U16, name="pos1_tile")
        pos2_tile = keep.tile([P, T // 16], U16, name="pos2_tile")
        bias = keep.tile([P, E], F32, name="bias")
        gates = keep.tile([P, 2, T], F32, name="gates")

        x_rows = xT.rearrange("(a p t) n -> a p t n", p=P, t=PACK)
        x_raw = []
        for a in range(A):
            raw = keep.tile([P, PACK, T], F32, name=f"x_raw_{a}")
            nc.sync.dma_start(out=raw[:], in_=x_rows[a])
            x_raw.append(raw)
            if a == 0:
                nc.sync.dma_start(offs_tile[:], offs)
        nc.sync.dma_start(out=bias[:], in_=b)
        w_rows = w.flatten_outer_dims().rearrange("(u p t) n -> p u (t n)", p=P, t=PACK)
        w_raw = []
        first = 0
        for i, shares in enumerate(W_GROUPS):
            blocks = sum(shares)
            tag = "reused" if i == REUSED_GROUP else f"w_raw_{i}"
            raw = keep.tile([P, blocks, PACK * N], F32, name=f"w_raw_{i}", tag=tag)
            nc.sync.dma_start(out=raw[:], in_=w_rows[:, first : first + blocks, :])
            w_raw.append(raw)
            first += blocks
            if i == POS_AFTER_GROUP:
                nc.sync.dma_start(pos1_tile[:], pos1)
                nc.sync.dma_start(pos2_tile[:], pos2)
        nc.sync.dma_start(out=gates[:], in_=gate.rearrange("r n t -> n r t"))

        x_scales = keep.tile([P, WINDOW], U8, name="x_scales", align_bytes=64)
        nc.gpsimd.memset(x_scales[:], 0)
        x_words = []
        for a in range(A):
            words = keep.tile([P, WINDOW], U32, name=f"x_words_{a}", align_bytes=64)
            nc.vector.memset(words[:, T:WINDOW].bitcast(I32), 0)
            x_words.append(words)

        slot_words = keep.tile([P, A, SLOTS], U32, name="slot_words", align_bytes=64)
        slot_scales = keep.tile([P, SLOTS], U8, name="slot_scales", align_bytes=64)
        for a in range(A):
            grouped = keep.tile([P, T, PACK], BF16, name=f"x_grouped_{a}", align_bytes=64)
            for engine, lo, hi in X_SHARES[a]:
                engine_copy[engine](
                    out=grouped[:, lo:hi, :].rearrange("p (c i) t -> p c t i", i=4),
                    in_=x_raw[a][:, :, lo:hi].rearrange("p t (c i) -> p c t i", i=4),
                )
            nc.vector.quantize_mx(
                out=x_words[a][:, 0:T].bitcast(FP8X4),
                scales=x_scales[SCALE_ROW * a : P, 0:T],
                in_=grouped[:].rearrange("p n t -> p (n t)"),
            )
            nc.vector.tensor_copy(slot_words[:, a, :], x_words[a][:].indirect(offs_tile[:]))
        nc.vector.tensor_copy(slot_scales[:], x_scales[:].indirect(offs_tile[:]))

        sums = []
        block = 0
        for i, (scalar_blocks, vector_blocks) in enumerate(W_GROUPS):
            blocks = scalar_blocks + vector_blocks
            grouped = keep.tile([P, blocks, N, PACK], BF16, name=f"w_grouped_{i}", align_bytes=64)
            for engine, lo, hi in (("scalar", 0, scalar_blocks), ("vector", scalar_blocks, blocks)):
                if lo < hi:
                    engine_copy[engine](
                        out=grouped[:, lo:hi].rearrange("p u (c i) t -> p u c t i", i=4),
                        in_=w_raw[i][:, lo:hi].rearrange("p u (t c i) -> p u c t i", t=PACK, i=4),
                    )
            w_words = keep.tile([P, blocks * N], U32, name=f"w_words_{i}", align_bytes=64)
            w_scales = keep.tile([P, blocks * N], U8, name=f"w_scales_{i}", align_bytes=64)
            nc.vector.quantize_mx(
                out=w_words[:].bitcast(FP8X4),
                scales=w_scales[:],
                in_=grouped[:].rearrange("p u n t -> p (u n t)"),
            )
            for j in range(blocks):
                e, a = divmod(block, A)
                if a == 0:
                    sums.append(psum.tile([N, C], F32, name=f"sums_{e}"))
                features = slice(j * N, (j + 1) * N)
                places = slice(e * C, (e + 1) * C)
                nc.tensor.matmul_mx(
                    out=sums[e][:],
                    lhsT=w_words[:, features].bitcast(FP8X4),
                    lhsT_scale=w_scales[:, features],
                    rhs=slot_words[:, a, places].bitcast(FP8X4),
                    rhs_scale=slot_scales[SCALE_ROW * a : P, places],
                    start=(a == 0),
                    stop=(a == A - 1),
                )
                block += 1

        results = keep.tile([P, SLOTS], F32, name="results", tag="reused")
        for e in range(E):
            places = slice(e * C, (e + 1) * C)
            if e < E - 1:
                nc.scalar.activation(results[:, places], sums[e][:], RELU, bias=bias[:, e : e + 1])
            else:
                nc.vector.tensor_scalar(results[:, places], sums[e][:], bias[:, e : e + 1], 0.0, ADD, MAX)

        y1 = keep.tile([P, T], F32, name="y1")
        nc.vector.tensor_tensor(y1[:], results[:].indirect(pos1_tile[:]), gates[:, 0, :], MULT)
        y2 = []
        for lo, hi in OUT_CUTS:
            part = keep.tile([P, hi - lo], F32, name=f"y2_{lo}")
            nc.vector.tensor_tensor(
                part[:], results[:].indirect(pos2_tile[:, lo // 16 : hi // 16]), gates[:, 1, lo:hi], MULT
            )
            y2.append(part)
        for (lo, hi), part in zip(OUT_CUTS, y2):
            y = keep.tile([P, hi - lo], F32, name=f"y_{lo}")
            nc.vector.tensor_tensor(y[:], y1[:, lo:hi], part[:], ADD)
            nc.sync.dma_start(out=out[:, lo:hi], in_=y[:])
